import numpy as np
import ml_dtypes

BF16 = ml_dtypes.bfloat16


def bf(x):
    return np.asarray(x, np.float32).astype(BF16)


def f32(x):
    return np.asarray(x, np.float32)


def f64(x):
    return np.asarray(x).astype(np.float64)


def striped(idx):
    return np.tile(idx.reshape(-1, 16).T, (8, 1))


def rows(idx, k):
    return np.tile(idx, (k, 1))


def look(tab, idx):
    return np.take_along_axis(f64(tab), rows(idx, len(tab)), axis=1)


K, S, V, N = 128, 2048, 1024, 1024


def silu(v):
    return v / (1.0 + np.exp(-v))


def setup_inputs():
    return {"tab": f32(np.random.standard_normal((2, K, S))), "offs": striped(np.random.permutation(S)[:N])}


def reference(tab, offs):
    idx = offs[:16].T.reshape(-1)
    x = (np.minimum(np.maximum(look(tab[0], idx), -1.25), 1.0)) * (silu(look(tab[1], idx)))
    return x

@@ -1,0 +1,39 @@
+import concourse.mybir as mybir
+
+ROWS = 128
+PLACES = 2048
+PICKED = 1024
+PER_COLUMN = 16
+PIECE = 512
+
+LOW, HIGH = -1.25, 1.0
+
+F32, U16 = mybir.dt.float32, mybir.dt.uint16
+MAX, MIN, MULT = mybir.AluOpType.max, mybir.AluOpType.min, mybir.AluOpType.mult
+SILU = mybir.ActivationFunctionType.Silu
+
+
+def tile_lookup_vg_clipsilu_out_kernel(tc, tab, offs, out):
+    nc = tc.nc
+    with tc.tile_pool(name="held", bufs=1) as held:
+        offsets = held.tile([ROWS, PICKED // PER_COLUMN], U16, name="offsets")
+        nc.sync.dma_start(offsets[:], offs)
+
+        values = held.tile([ROWS, PLACES], F32, name="values")
+        gates = held.tile([ROWS, PLACES], F32, name="gates")
+        nc.sync.dma_start(values[:], tab[0])
+        nc.sync.dma_start(gates[:], tab[1])
+
+        clamped = held.tile([ROWS, PICKED], F32, name="clamped")
+        nc.vector.tensor_scalar(clamped[:], values[:].indirect(offsets[:]), LOW, HIGH, MAX, MIN)
+
+        for piece in range(PICKED // PIECE):
+            here = slice(piece * PIECE, (piece + 1) * PIECE)
+            columns = slice(piece * PIECE // PER_COLUMN, (piece + 1) * PIECE // PER_COLUMN)
+
+            opened = held.tile([ROWS, PIECE], F32, name="opened%d" % piece)
+            nc.scalar.activation(opened[:], gates[:].indirect(offsets[:, columns]), SILU)
+
+            product = held.tile([ROWS, PIECE], F32, name="product%d" % piece)
+            nc.vector.tensor_tensor(product[:], clamped[:, here], opened[:], MULT)
+            nc.sync.dma_start(out[:, here], product[:])

@@ -19,6 +19,11 @@ def tile_lookup_vg_clipsilu_out_kernel(tc, tab, offs, out):
         offsets = held.tile([ROWS, PICKED // PER_COLUMN], U16, name="offsets")
         nc.sync.dma_start(offsets[:], offs)
 
+        zero = held.tile([ROWS, 1], F32, name="zero")
+        silu_of_zero = held.tile([ROWS, 1], F32, name="silu_of_zero")
+        nc.vector.memset(zero[:], 0.0)
+        nc.scalar.activation(silu_of_zero[:], zero[:], SILU)
+
         values = held.tile([ROWS, PLACES], F32, name="values")
         gates = held.tile([ROWS, PLACES], F32, name="gates")
         nc.sync.dma_start(values[:], tab[0])

@@ -5,6 +5,7 @@ PLACES = 2048
 PICKED = 1024
 PER_COLUMN = 16
 PIECE = 512
+STRIP = 256
 
 LOW, HIGH = -1.25, 1.0
 
@@ -33,12 +34,15 @@ def tile_lookup_vg_clipsilu_out_kernel(tc, tab, offs, out):
         nc.vector.tensor_scalar(clamped[:], values[:].indirect(offsets[:]), LOW, HIGH, MAX, MIN)
 
         for piece in range(PICKED // PIECE):
-            here = slice(piece * PIECE, (piece + 1) * PIECE)
             columns = slice(piece * PIECE // PER_COLUMN, (piece + 1) * PIECE // PER_COLUMN)
 
             opened = held.tile([ROWS, PIECE], F32, name="opened%d" % piece)
             nc.scalar.activation(opened[:], gates[:].indirect(offsets[:, columns]), SILU)
 
-            product = held.tile([ROWS, PIECE], F32, name="product%d" % piece)
-            nc.vector.tensor_tensor(product[:], clamped[:, here], opened[:], MULT)
-            nc.sync.dma_start(out[:, here], product[:])
+            for strip in range(PIECE // STRIP):
+                inside = slice(strip * STRIP, (strip + 1) * STRIP)
+                start = piece * PIECE + strip * STRIP
+                overall = slice(start, start + STRIP)
+                product = held.tile([ROWS, STRIP], F32, name="product%d_%d" % (piece, strip))
+                nc.vector.tensor_tensor(product[:], clamped[:, overall], opened[:, inside], MULT)
+                nc.sync.dma_start(out[:, overall], product[:])

import concourse.mybir as mybir

ROWS = 128
PLACES = 2048
PICKED = 1024
PER_COLUMN = 16
PIECE = 512
STRIP = 256

LOW, HIGH = -1.25, 1.0

F32, U16 = mybir.dt.float32, mybir.dt.uint16
MAX, MIN, MULT = mybir.AluOpType.max, mybir.AluOpType.min, mybir.AluOpType.mult
SILU = mybir.ActivationFunctionType.Silu


def tile_lookup_vg_clipsilu_out_kernel(tc, tab, offs, out):
    nc = tc.nc
    with tc.tile_pool(name="held", bufs=1) as held:
        offsets = held.tile([ROWS, PICKED // PER_COLUMN], U16, name="offsets")
        nc.sync.dma_start(offsets[:], offs)

        zero = held.tile([ROWS, 1], F32, name="zero")
        silu_of_zero = held.tile([ROWS, 1], F32, name="silu_of_zero")
        nc.vector.memset(zero[:], 0.0)
        nc.scalar.activation(silu_of_zero[:], zero[:], SILU)

        values = held.tile([ROWS, PLACES], F32, name="values")
        gates = held.tile([ROWS, PLACES], F32, name="gates")
        nc.sync.dma_start(values[:], tab[0])
        nc.sync.dma_start(gates[:], tab[1])

        clamped = held.tile([ROWS, PICKED], F32, name="clamped")
        nc.vector.tensor_scalar(clamped[:], values[:].indirect(offsets[:]), LOW, HIGH, MAX, MIN)

        for piece in range(PICKED // PIECE):
            columns = slice(piece * PIECE // PER_COLUMN, (piece + 1) * PIECE // PER_COLUMN)

            opened = held.tile([ROWS, PIECE], F32, name="opened%d" % piece)
            nc.scalar.activation(opened[:], gates[:].indirect(offsets[:, columns]), SILU)

            for strip in range(PIECE // STRIP):
                inside = slice(strip * STRIP, (strip + 1) * STRIP)
                start = piece * PIECE + strip * STRIP
                overall = slice(start, start + STRIP)
                product = held.tile([ROWS, STRIP], F32, name="product%d_%d" % (piece, strip))
                nc.vector.tensor_tensor(product[:], clamped[:, overall], opened[:, inside], MULT)
                nc.sync.dma_start(out[:, overall], product[:])
